import numpy as np
import ml_dtypes


def mxq(x, axis, fmt="e4m3"):
    dtype, down = {"e4m3": (ml_dtypes.float8_e4m3fn, 7), "e5m2": (ml_dtypes.float8_e5m2, 14)}[fmt]
    v = np.moveaxis(np.asarray(x, np.float32).astype(ml_dtypes.bfloat16).astype(np.float64), axis, -1)
    blocks = v.reshape(v.shape[:-1] + (-1, 32))
    amax = np.abs(blocks).max(-1, keepdims=True)
    byte = np.maximum(np.where(amax > 0, np.frexp(amax)[1] - 1 + 127, 0) - down, 1)
    scale = np.exp2(byte - 127.0)
    codes = (blocks / scale).astype(np.float32).astype(dtype).astype(np.float64)
    return np.moveaxis((codes * scale).reshape(v.shape), -1, axis)


WIDE = False


def mx_kscale(k):
    if not WIDE:
        return np.ones(k)
    levels = np.array([10, -10, 5, -5, 0])
    if k % 512:
        return np.exp2(np.random.permutation(np.resize(levels, k // 32))).repeat(32)
    a = np.empty((k // 512, 16))
    for p in range(k // 512):
        a[p, :8] = np.random.permutation(np.resize(levels, 8))
        for g in range(8):
            far = levels[np.abs(levels - a[p, g]) >= 10]
            a[p, g + 8] = far[np.random.randint(len(far))]
    return np.exp2(a.ravel()).repeat(32)


def f64(x):
    return np.asarray(x).astype(np.float64)


def striped(idx):
    return np.tile(np.asarray(idx).reshape(-1, 16).T, (8, 1)).astype(np.uint16)


def unstriped(offs):
    return offs[:16].T.reshape(-1).astype(np.int64)


E2M1 = np.array([0.0, 0.5, 1.0, 1.5, 2.0, 3.0, 4.0, 6.0, -0.0, -0.5, -1.0, -1.5, -2.0, -3.0, -4.0, -6.0])


def pack_weight(w, fmt):
    k, n = w.shape
    w = f64(np.asarray(w, np.float32).astype(ml_dtypes.bfloat16)).reshape(k // 32, 32, n)
    amax = np.abs(w).max(1)
    if fmt == "e4m3":
        byte = np.frexp(amax)[1] - 1 + 127 - 7
    else:
        mant, ex = np.frexp(amax / 6.0)
        byte = np.where(mant > 0.5, ex, ex - 1) + 127
    byte = np.clip(np.where(amax > 0, byte, 1), 1, 254)
    scaled = (w * np.exp2(127.0 - byte)[:, None, :]).reshape(k, n).astype(np.float32)
    by_word = np.ascontiguousarray(scaled.reshape(k // 512, 128, 4, n).transpose(0, 1, 3, 2))
    if fmt == "e4m3":
        words = by_word.astype(ml_dtypes.float8_e4m3fn).view(np.uint8)
    else:
        c = by_word.astype(ml_dtypes.float4_e2m1fn).view(np.uint8) & 0xF
        words = (c[..., 0::2] | (c[..., 1::2] << 4)).reshape(k // 512, 128, 2 * n)
    return np.ascontiguousarray(words), np.ascontiguousarray(byte.astype(np.uint8).reshape(k // 512, 16, n))


def unpack_weight(words, scales, fmt):
    g, _, n = scales.shape
    words = np.ascontiguousarray(words).reshape(g, 128, n, -1)
    if fmt == "e4m3":
        vals = words.view(ml_dtypes.float8_e4m3fn).astype(np.float64)
    else:
        nib = np.empty((g, 128, n, 4), np.uint8)
        nib[..., 0::2] = words & 0xF
        nib[..., 1::2] = words >> 4
        vals = E2M1[nib]
    vals = vals * np.repeat(np.exp2(scales.astype(np.float64) - 127.0), 8, axis=1)[..., None]
    return vals.transpose(0, 1, 3, 2).reshape(g * 512, n)


D, T, I, Q, E, X = 512, 2048, 512, 128, 512, 1024


def setup_inputs():
    n = np.random.standard_normal
    idx = np.random.permutation(T)[:I]
    idx2 = np.random.permutation(T)[:I]
    idx3 = np.random.permutation(X)[:I]
    fd = mx_kscale(D)
    fi = mx_kscale(I)
    ti = np.ones(T)
    ti[idx] = fi
    ti3 = np.ones(X)
    ti3[idx3] = fi
    keysp = pack_weight(n((D, T)) / fd[:, None], "e4m3")
    return {
        "query": (n((D, Q)) * 1.0 / np.sqrt(D) * fd[:, None]).astype(np.float32),
        "query2": (n((D, Q)) * 1.0 / np.sqrt(D) * fd[:, None]).astype(np.float32),
        "keys_words": keysp[0],
        "keys_scales": keysp[1],
        "lam": (np.random.uniform(1.0, 3.0, (Q, 1))).astype(np.float32),
        "pull": (np.random.uniform(0.3, 0.9, (Q, 1))).astype(np.float32),
        "os": (np.random.uniform(4.0, 16.0, (1, I)) * fi).astype(np.float32),
        "vals": (n((E, T)) / ti).astype(np.float32),
        "vals2": (n((E, X)) / ti3).astype(np.float32),
        "offs": striped(idx),
        "offs2": striped(idx2),
        "offs3": striped(idx3),
    }


def reference(query, query2, keys_words, keys_scales, lam, pull, os, vals, vals2, offs, offs2, offs3):
    idx = unstriped(offs)
    idx2 = unstriped(offs2)
    idx3 = unstriped(offs3)
    keysu = unpack_weight(keys_words, keys_scales, "e4m3")
    queryq = mxq(f64(query), 0, "e4m3")
    a = queryq.T @ keysu
    query2q = mxq(f64(query2), 0, "e4m3")
    b = query2q.T @ keysu
    la = np.square(a[:, idx]) + np.square(b[:, idx])
    lb = np.square(a[:, idx2]) + np.square(b[:, idx2])
    s = (a[:, idx] * a[:, idx2] + b[:, idx] * b[:, idx2]) / np.sqrt(la * lb + 0.5) * f64(lam)
    p = np.exp(s - np.max(s, axis=1, keepdims=True))
    r = p / np.sum(p, axis=1, keepdims=True)
    r1 = np.pad(r, ((0, 0), (1, 0)))[:, :I]
    w = r - r1 * f64(pull)
    wo1 = np.maximum(w, 0.0) * f64(os)
    wo2 = np.maximum(w * (-1.0), 0.0) * f64(os)
    wt1 = wo1.T
    wt2 = wo2.T
    vt1 = f64(vals)[:, idx].T
    vt2 = f64(vals2)[:, idx3].T
    wt1q = mxq(wt1, 0, "e4m3")
    vt1q = mxq(vt1, 0, "e4m3")
    o = wt1q.T @ vt1q
    wt2q = mxq(wt2, 0, "e4m3")
    vt2q = mxq(vt2, 0, "e4m3")
    o2 = wt2q.T @ vt2q
    y = o - o2
    return y

@@ -1,0 +1,222 @@
+from contextlib import ExitStack
+
+import concourse.mybir as mybir
+from concourse.masks import make_identity
+
+D, T, I, Q, E, X = 512, 2048, 512, 128, 512, 1024
+FLOPS = 2 * (2 * D * Q * T + 2 * I * Q * E)
+
+F32 = mybir.dt.float32
+BF16 = mybir.dt.bfloat16
+I32 = mybir.dt.int32
+U32 = mybir.dt.uint32
+U16 = mybir.dt.uint16
+U8 = mybir.dt.uint8
+FP8X4 = mybir.dt.float8_e4m3fn_x4
+ALU = mybir.AluOpType
+ACT = mybir.ActivationFunctionType
+
+P = 128
+PACK = 4
+BANK = 512
+PAD = 8
+WINDOW_BYTES = T * 4
+
+
+def tile_attend_planecos_stepwise_bysign_kernel(
+    tc, query, query2, keys_words, keys_scales, lam, pull, slot_factor, vals, vals2, offs, offs2, offs3, out
+):
+    nc = tc.nc
+    with ExitStack() as ctx:
+        keep = ctx.enter_context(tc.tile_pool(name="keep", bufs=1))
+        shared = ctx.enter_context(tc.tile_pool(name="shared", bufs=1))
+        banks = ctx.enter_context(tc.psum_pool(name="banks", bufs=4))
+        turns = ctx.enter_context(tc.psum_pool(name="turns", bufs=2))
+        single = ctx.enter_context(tc.psum_pool(name="single", bufs=1))
+
+        def sbuf(name, shape, dtype):
+            return keep.tile(shape, dtype, name=name, align_bytes=64)
+
+        def after_gather(block, at, name, shape, dtype):
+            return shared.tile(shape, dtype, name=name, align_bytes=64, offset=block * WINDOW_BYTES + at)
+
+        key_scales = sbuf("key_scales", [P, BANK], U8)
+        nc.gpsimd.memset(key_scales[:].bitcast(I32), 0)
+        warm = sbuf("warm", [P, 1], F32)
+        nc.gpsimd.memset(warm[:], 1.0)
+
+        half = T // 2
+        key_bytes = keys_words[0].rearrange("p n t -> p (n t)")
+        key_words = [sbuf("key_words%d" % n, [P, half], U32) for n in range(2)]
+        q_raw = [sbuf("q_raw%d" % n, [P, PACK, Q], F32) for n in range(2)]
+        nc.sync.dma_start(out=q_raw[0][:], in_=query.rearrange("(p j) w -> p j w", j=PACK))
+        for quad in range(4):
+            (nc.sync, nc.scalar)[quad % 2].dma_start(
+                out=key_scales[32 * quad : 32 * quad + 16, :].bitcast(I32),
+                in_=keys_scales[0, 4 * quad : 4 * quad + 4, :].rearrange("j (c n) -> c j n", c=4).bitcast(I32),
+            )
+        warm_out = sbuf("warm_out", [P, 1], F32)
+        nc.scalar.activation(warm_out[:], warm[:], ACT.Abs_reciprocal_sqrt)
+        for n in range(2):
+            nc.sync.dma_start(
+                out=key_words[n][:].bitcast(I32),
+                in_=key_bytes[:, n * half * PACK : (n + 1) * half * PACK].bitcast(I32),
+            )
+        nc.sync.dma_start(out=q_raw[1][:], in_=query2.rearrange("(p j) w -> p j w", j=PACK))
+
+        lam_col = sbuf("lam_col", [P, 1], F32)
+        pull_col = sbuf("pull_col", [P, 1], F32)
+        os_rows = sbuf("os_rows", [P, PACK], F32)
+        ident = sbuf("ident", [P, P], F32)
+        make_identity(nc, ident[:])
+        nc.gpsimd.dma_start(out=os_rows[:], in_=slot_factor.rearrange("o (p t) -> (o p) t", t=PACK))
+        nc.gpsimd.dma_start(out=lam_col[:], in_=lam)
+        nc.gpsimd.dma_start(out=pull_col[:], in_=pull)
+
+        lists = [sbuf("list%d" % n, [P, I // 16], U16) for n in range(3)]
+        pool1 = [after_gather(n, 0, "pool1_%d" % n, [P, T], F32) for n in range(4)]
+        pool2 = [sbuf("pool2_%d" % n, [P, X], F32) for n in range(4)]
+        nc.sync.dma_start(lists[0][:], offs)
+        nc.sync.dma_start(lists[1][:], offs2)
+        nc.sync.dma_start(out=pool2[0][:], in_=vals2[0:P, :])
+        nc.sync.dma_start(lists[2][:], offs3)
+        for n in range(1, 4):
+            nc.sync.dma_start(out=pool2[n][:], in_=vals2[n * P : (n + 1) * P, :])
+        for n in range(4):
+            nc.sync.dma_start(out=pool1[n][:], in_=vals[n * P : (n + 1) * P, :])
+
+        q_codes, q_scales = [], []
+        for n in range(2):
+            grouped = sbuf("q_grouped%d" % n, [P, Q * PACK], BF16)
+            nc.vector.tensor_copy(
+                out=grouped[:].rearrange("p (w j) -> p w j", j=PACK), in_=q_raw[n][:].rearrange("p j w -> p w j")
+            )
+            codes = sbuf("q_codes%d" % n, [P, Q], U32)
+            scales = sbuf("q_scales%d" % n, [P, Q], U8)
+            nc.vector.quantize_mx(out=codes[:].bitcast(FP8X4), scales=scales[:], in_=grouped[:])
+            q_codes.append(codes)
+            q_scales.append(scales)
+
+        planes = [after_gather(4 + n, 0, "plane%d" % n, [P, T], F32) for n in range(2)]
+        for n in range(2):
+            for c in range(T // BANK):
+                acc = banks.tile([P, BANK], F32, name="acc")
+                within = (c % 2) * BANK
+                nc.tensor.matmul_mx(
+                    out=acc[:],
+                    lhsT=q_codes[n][:].bitcast(FP8X4),
+                    lhsT_scale=q_scales[n][:],
+                    rhs=key_words[c // 2][:, within : within + BANK].bitcast(FP8X4),
+                    rhs_scale=key_scales[4 * c :, :],
+                    start=True,
+                    stop=True,
+                )
+                nc.scalar.copy(out=planes[n][:, c * BANK : (c + 1) * BANK], in_=acc[:])
+
+        os_bank = banks.tile([P, PACK, P], F32, name="acc")
+        for t in range(PACK):
+            nc.tensor.transpose(os_bank[:, t, :], os_rows[:, t : t + 1].to_broadcast([P, P]), ident[:])
+
+        v_grouped = [sbuf("v_grouped%d" % n, [P, E * PACK], BF16) for n in range(2)]
+
+        def turn(dst_bf16, src_bf16, bank):
+            words = src_bf16.bitcast(F32)
+            for u in range(2):
+                nc.tensor.transpose(bank[:, u, :], words[:, u : I // 2 : 2], ident[:])
+            nc.scalar.copy(
+                out=dst_bf16.bitcast(F32).rearrange("p (r u) -> p r u", u=2), in_=bank.rearrange("p u r -> p r u")
+            )
+
+        def values(n, block):
+            window = (pool1, pool2)[n][block]
+            picked = after_gather(5, (4 * n + block) * I * 2, "picked%d_%d" % (n, block), [P, I], BF16)
+            nc.vector.tensor_copy(out=picked[:], in_=window[:].indirect(lists[2 * n][:]))
+            bank = turns.tile([P, 2, P], F32, name="turned")
+            turn(v_grouped[n][:, block * P * PACK : (block + 1) * P * PACK], picked[:], bank[:])
+
+        def work(name):
+            return sbuf(name, [P, I], F32)
+
+        a1, a2, b1, b2 = work("a1"), work("a2"), work("b1"), work("b2")
+        sq_a1, sq_a2, sq_b1, sq_b2 = work("sq_a1"), work("sq_a2"), work("sq_b1"), work("sq_b2")
+        for dst, sq, plane, lst in ((a1, sq_a1, 0, 0), (a2, sq_a2, 0, 1), (b1, sq_b1, 1, 0), (b2, sq_b2, 1, 1)):
+            nc.vector.tensor_copy(out=dst[:], in_=planes[plane][:].indirect(lists[lst][:]))
+            nc.scalar.activation(sq[:], dst[:], ACT.Square)
+        aa, bb, la, lb, dot, prod = work("aa"), work("bb"), work("la"), work("lb"), work("dot"), work("prod")
+        nc.gpsimd.tensor_tensor(aa[:], a1[:], a2[:], ALU.mult)
+        nc.gpsimd.tensor_tensor(la[:], sq_a1[:], sq_b1[:], ALU.add)
+        nc.gpsimd.tensor_tensor(lb[:], sq_a2[:], sq_b2[:], ALU.add)
+        nc.gpsimd.tensor_tensor(prod[:], la[:], lb[:], ALU.mult)
+        nc.gpsimd.tensor_tensor(bb[:], b1[:], b2[:], ALU.mult)
+        nc.gpsimd.tensor_tensor(dot[:], aa[:], bb[:], ALU.add)
+        inv_len = work("inv_len")
+        nc.scalar.activation(inv_len[:], prod[:], ACT.Abs_reciprocal_sqrt, bias=0.5)
+        warm_exp = sbuf("warm_exp", [P, 1], F32)
+        nc.scalar.activation(warm_exp[:], inv_len[:, 0:1], ACT.Exp)
+
+        for block in range(4):
+            values(1, block)
+        values(0, 0)
+        v2_codes = after_gather(0, 0, "v2_codes", [P, E], U32)
+        v2_scales = after_gather(0, 2048, "v2_scales", [P, E], U8)
+        nc.vector.quantize_mx(out=v2_codes[:].bitcast(FP8X4), scales=v2_scales[:], in_=v_grouped[1][:])
+
+        score = after_gather(0, 4096, "score", [P, I], F32)
+        nc.vector.scalar_tensor_tensor(score[:], dot[:], lam_col[:], inv_len[:], ALU.mult, ALU.mult)
+        neg_max = sbuf("neg_max", [P, 1], F32)
+        nc.vector.tensor_reduce(neg_max[:], score[:], mybir.AxisListType.X, ALU.max, negate=True)
+
+        shares = sbuf("shares", [P, PAD + I], F32)
+        nc.gpsimd.memset(shares[:, PAD - 1 : PAD], 0.0)
+        row_sum = sbuf("row_sum", [P, 1], F32)
+        nc.scalar.activation(shares[:, PAD:], score[:], ACT.Exp, bias=neg_max[:], accum_out=row_sum[:])
+        values(0, 1)
+        inv_sum = after_gather(1, 0, "inv_sum", [P, 1], F32)
+        nc.vector.reciprocal(inv_sum[:], row_sum[:])
+        factor = work("factor")
+        nc.scalar.activation(
+            factor[:].rearrange("p (s t) -> p s t", t=PACK),
+            os_bank[:].rearrange("p t s -> p s t"),
+            ACT.Copy,
+            scale=inv_sum[:],
+        )
+        neg_step = after_gather(1, 2048, "neg_step", [P, I], F32)
+        nc.vector.scalar_tensor_tensor(
+            neg_step[:], shares[:, PAD - 1 : PAD - 1 + I], pull_col[:], shares[:, PAD:], ALU.mult, ALU.subtract
+        )
+        w_grouped = sbuf("w_grouped", [P, 2 * Q * PACK], BF16)
+        for n, op in enumerate((ALU.min, ALU.max)):
+            weights = sbuf("weights%d" % n, [P, I], BF16)
+            nc.vector.scalar_tensor_tensor(weights[:], neg_step[:], 0.0, factor[:], op, ALU.mult)
+            w_bank = banks.tile([P, 2, P], F32, name="acc")
+            turn(w_grouped[:, n * Q * PACK : (n + 1) * Q * PACK], weights[:], w_bank[:])
+        values(0, 2)
+        values(0, 3)
+        w_codes = after_gather(3, 0, "w_codes", [P, 2 * Q], U32)
+        w_scales = after_gather(3, 2048, "w_scales", [P, 2 * Q], U8)
+        nc.vector.quantize_mx(out=w_codes[:].bitcast(FP8X4), scales=w_scales[:], in_=w_grouped[:])
+
+        width = E // 2
+        for part in range(2):
+            cols = slice(part * width, (part + 1) * width)
+            v1_codes = after_gather(3, 4096 + 2048 * part, "v1_codes%d" % part, [P, width], U32)
+            v1_scales = after_gather(3, 5120 + 2048 * part, "v1_scales%d" % part, [P, width], U8)
+            nc.vector.quantize_mx(
+                out=v1_codes[:].bitcast(FP8X4),
+                scales=v1_scales[:],
+                in_=v_grouped[0][:, part * width * PACK : (part + 1) * width * PACK],
+            )
+            acc = single.tile([P, width], F32, name="result_bank%d" % part)
+            for n, codes, scales in ((1, v2_codes[:, cols], v2_scales[:, cols]), (0, v1_codes[:], v1_scales[:])):
+                nc.tensor.matmul_mx(
+                    out=acc[:],
+                    lhsT=w_codes[:, n * Q : (n + 1) * Q].bitcast(FP8X4),
+                    lhsT_scale=w_scales[:, n * Q : (n + 1) * Q],
+                    rhs=codes.bitcast(FP8X4),
+                    rhs_scale=scales,
+                    start=(n == 1),
+                    stop=(n == 0),
+                )
+            result = sbuf("result%d" % part, [P, width], F32)
+            nc.scalar.activation(result[:], acc[:], ACT.Copy, scale=-1.0)
+            nc.sync.dma_start(out=out[:, cols], in_=result[:])

@@ -20,7 +20,6 @@ P = 128
 PACK = 4
 BANK = 512
 PAD = 8
-WINDOW_BYTES = T * 4
 
 
 def tile_attend_planecos_stepwise_bysign_kernel(
@@ -29,16 +28,16 @@ def tile_attend_planecos_stepwise_bysign_kernel(
     nc = tc.nc
     with ExitStack() as ctx:
         keep = ctx.enter_context(tc.tile_pool(name="keep", bufs=1))
-        shared = ctx.enter_context(tc.tile_pool(name="shared", bufs=1))
-        banks = ctx.enter_context(tc.psum_pool(name="banks", bufs=4))
-        turns = ctx.enter_context(tc.psum_pool(name="turns", bufs=2))
-        single = ctx.enter_context(tc.psum_pool(name="single", bufs=1))
+        psum = ctx.enter_context(tc.psum_pool(name="psum", bufs=1))
 
-        def sbuf(name, shape, dtype):
-            return keep.tile(shape, dtype, name=name, align_bytes=64)
+        def sbuf(name, shape, dtype, tag=None):
+            return keep.tile(shape, dtype, name=name, tag=tag or name, align_bytes=64)
 
-        def after_gather(block, at, name, shape, dtype):
-            return shared.tile(shape, dtype, name=name, align_bytes=64, offset=block * WINDOW_BYTES + at)
+        def bank(number, name, shape):
+            return psum.tile(shape, F32, name=name, tag="bank%d" % number)
+
+        def work(name, tag=None):
+            return sbuf(name, [P, I], F32, tag)
 
         key_scales = sbuf("key_scales", [P, BANK], U8)
         nc.gpsimd.memset(key_scales[:].bitcast(I32), 0)
@@ -74,12 +73,12 @@ def tile_attend_planecos_stepwise_bysign_kernel(
         nc.gpsimd.dma_start(out=pull_col[:], in_=pull)
 
         lists = [sbuf("list%d" % n, [P, I // 16], U16) for n in range(3)]
-        pool1 = [after_gather(n, 0, "pool1_%d" % n, [P, T], F32) for n in range(4)]
+        pool1 = [sbuf("pool1_%d" % n, [P, T], F32) for n in range(4)]
         pool2 = [sbuf("pool2_%d" % n, [P, X], F32) for n in range(4)]
-        nc.sync.dma_start(lists[0][:], offs)
-        nc.sync.dma_start(lists[1][:], offs2)
         nc.sync.dma_start(out=pool2[0][:], in_=vals2[0:P, :])
         nc.sync.dma_start(lists[2][:], offs3)
+        nc.sync.dma_start(lists[0][:], offs)
+        nc.sync.dma_start(lists[1][:], offs2)
         for n in range(1, 4):
             nc.sync.dma_start(out=pool2[n][:], in_=vals2[n * P : (n + 1) * P, :])
         for n in range(4):
@@ -97,10 +96,10 @@ def tile_attend_planecos_stepwise_bysign_kernel(
             q_codes.append(codes)
             q_scales.append(scales)
 
-        planes = [after_gather(4 + n, 0, "plane%d" % n, [P, T], F32) for n in range(2)]
+        planes = [sbuf("plane%d" % n, [P, T], F32) for n in range(2)]
         for n in range(2):
             for c in range(T // BANK):
-                acc = banks.tile([P, BANK], F32, name="acc")
+                acc = bank(4 * n + c, "plane_bank%d_%d" % (n, c), [P, BANK])
                 within = (c % 2) * BANK
                 nc.tensor.matmul_mx(
                     out=acc[:],
@@ -113,66 +112,98 @@ def tile_attend_planecos_stepwise_bysign_kernel(
                 )
                 nc.scalar.copy(out=planes[n][:, c * BANK : (c + 1) * BANK], in_=acc[:])
 
-        os_bank = banks.tile([P, PACK, P], F32, name="acc")
-        for t in range(PACK):
-            nc.tensor.transpose(os_bank[:, t, :], os_rows[:, t : t + 1].to_broadcast([P, P]), ident[:])
-
         v_grouped = [sbuf("v_grouped%d" % n, [P, E * PACK], BF16) for n in range(2)]
 
-        def turn(dst_bf16, src_bf16, bank):
+        def turn(dst_bf16, src_bf16, turned):
             words = src_bf16.bitcast(F32)
             for u in range(2):
-                nc.tensor.transpose(bank[:, u, :], words[:, u : I // 2 : 2], ident[:])
+                nc.tensor.transpose(turned[:, u, :], words[:, u : I // 2 : 2], ident[:])
             nc.scalar.copy(
-                out=dst_bf16.bitcast(F32).rearrange("p (r u) -> p r u", u=2), in_=bank.rearrange("p u r -> p r u")
+                out=dst_bf16.bitcast(F32).rearrange("p (r u) -> p r u", u=2), in_=turned.rearrange("p u r -> p r u")
             )
 
-        def values(n, block):
+        def pick(n, block, tag=None, into=None):
             window = (pool1, pool2)[n][block]
-            picked = after_gather(5, (4 * n + block) * I * 2, "picked%d_%d" % (n, block), [P, I], BF16)
-            nc.vector.tensor_copy(out=picked[:], in_=window[:].indirect(lists[2 * n][:]))
-            bank = turns.tile([P, 2, P], F32, name="turned")
-            turn(v_grouped[n][:, block * P * PACK : (block + 1) * P * PACK], picked[:], bank[:])
+            picked = sbuf("picked%d_%d" % (n, block), [P, I], BF16, tag)[:] if into is None else into
+            nc.vector.tensor_copy(out=picked, in_=window[:].indirect(lists[2 * n][:]))
+            return picked
 
-        def work(name):
-            return sbuf(name, [P, I], F32)
+        def lay(n, block, picked, number):
+            turned = bank(number, "turned%d_%d" % (n, block), [P, 2, P])
+            turn(v_grouped[n][:, block * P * PACK : (block + 1) * P * PACK], picked, turned[:])
 
-        a1, a2, b1, b2 = work("a1"), work("a2"), work("b1"), work("b2")
-        sq_a1, sq_a2, sq_b1, sq_b2 = work("sq_a1"), work("sq_a2"), work("sq_b1"), work("sq_b2")
-        for dst, sq, plane, lst in ((a1, sq_a1, 0, 0), (a2, sq_a2, 0, 1), (b1, sq_b1, 1, 0), (b2, sq_b2, 1, 1)):
-            nc.vector.tensor_copy(out=dst[:], in_=planes[plane][:].indirect(lists[lst][:]))
-            nc.scalar.activation(sq[:], dst[:], ACT.Square)
-        aa, bb, la, lb, dot, prod = work("aa"), work("bb"), work("la"), work("lb"), work("dot"), work("prod")
-        nc.gpsimd.tensor_tensor(aa[:], a1[:], a2[:], ALU.mult)
-        nc.gpsimd.tensor_tensor(la[:], sq_a1[:], sq_b1[:], ALU.add)
-        nc.gpsimd.tensor_tensor(lb[:], sq_a2[:], sq_b2[:], ALU.add)
-        nc.gpsimd.tensor_tensor(prod[:], la[:], lb[:], ALU.mult)
-        nc.gpsimd.tensor_tensor(bb[:], b1[:], b2[:], ALU.mult)
-        nc.gpsimd.tensor_tensor(dot[:], aa[:], bb[:], ALU.add)
+        def add_turned(total, part, first, last):
+            for j in range(I // P):
+                nc.tensor.matmul(
+                    total[:, j * P : (j + 1) * P],
+                    lhsT=part[:, j * P : (j + 1) * P],
+                    rhs=ident[:],
+                    is_transpose=True,
+                    start=(first and j == 0),
+                    stop=(last and j == I // P - 1),
+                )
+
+        lay(1, 0, pick(1, 0), 4)
+
+        la_bank, lb_bank, dot_bank = bank(0, "la_bank", [P, I]), bank(1, "lb_bank", [P, I]), bank(2, "dot_bank", [P, I])
+        points = {}
+        for plane, lst in ((0, 0), (0, 1), (1, 0), (1, 1)):
+            point = work("point%d_%d" % (plane, lst))
+            nc.vector.tensor_copy(out=point[:], in_=planes[plane][:].indirect(lists[lst][:]))
+            square = work("square%d_%d" % (plane, lst))
+            nc.scalar.activation(square[:], point[:], ACT.Square)
+            add_turned((la_bank, lb_bank)[lst], square, plane == 0, plane == 1)
+            points[plane, lst] = point
+            if lst == 1:
+                product = work("product%d" % plane)
+                nc.gpsimd.tensor_tensor(product[:], points[plane, 0][:], point[:], ALU.mult)
+                add_turned(dot_bank, product, plane == 0, plane == 1)
+        la = work("la")
+        nc.scalar.copy(out=la[:], in_=la_bank[:])
+
+        pair = sbuf("pair", [P, 2 * I], BF16, "plane1")
+        picked21 = pick(1, 1, into=pair[:, :I])
+        picked22 = pick(1, 2, into=pair[:, I:])
+        prod = work("prod")
+        nc.vector.tensor_tensor(prod[:], lb_bank[:], la[:], ALU.mult)
+        picked23 = pick(1, 3, "square1_1")
         inv_len = work("inv_len")
         nc.scalar.activation(inv_len[:], prod[:], ACT.Abs_reciprocal_sqrt, bias=0.5)
         warm_exp = sbuf("warm_exp", [P, 1], F32)
         nc.scalar.activation(warm_exp[:], inv_len[:, 0:1], ACT.Exp)
+        lay(1, 1, picked21, 0)
+        lay(1, 2, picked22, 1)
 
-        for block in range(4):
-            values(1, block)
-        values(0, 0)
-        v2_codes = after_gather(0, 0, "v2_codes", [P, E], U32)
-        v2_scales = after_gather(0, 2048, "v2_scales", [P, E], U8)
-        nc.vector.quantize_mx(out=v2_codes[:].bitcast(FP8X4), scales=v2_scales[:], in_=v_grouped[1][:])
-
-        score = after_gather(0, 4096, "score", [P, I], F32)
-        nc.vector.scalar_tensor_tensor(score[:], dot[:], lam_col[:], inv_len[:], ALU.mult, ALU.mult)
+        cosine = work("cosine")
+        nc.vector.tensor_tensor(cosine[:], dot_bank[:], inv_len[:], ALU.mult)
+        picked10 = pick(0, 0, "prod")
+        cos_bank = bank(5, "cos_bank", [P, I])
+        add_turned(cos_bank, cosine, True, True)
+        lay(1, 3, picked23, 2)
+        neg_lam = sbuf("neg_lam", [P, 1], F32)
+        nc.gpsimd.tensor_scalar(neg_lam[:], lam_col[:], -1.0, 0.0, ALU.mult, ALU.add)
+        neg_score = work("neg_score")
         neg_max = sbuf("neg_max", [P, 1], F32)
-        nc.vector.tensor_reduce(neg_max[:], score[:], mybir.AxisListType.X, ALU.max, negate=True)
+        nc.vector.tensor_scalar(neg_score[:], cos_bank[:], neg_lam[:], None, ALU.mult, ALU.min, accum_out=neg_max[:])
+        picked11 = pick(0, 1, "cosine")
 
         shares = sbuf("shares", [P, PAD + I], F32)
         nc.gpsimd.memset(shares[:, PAD - 1 : PAD], 0.0)
         row_sum = sbuf("row_sum", [P, 1], F32)
-        nc.scalar.activation(shares[:, PAD:], score[:], ACT.Exp, bias=neg_max[:], accum_out=row_sum[:])
-        values(0, 1)
-        inv_sum = after_gather(1, 0, "inv_sum", [P, 1], F32)
+        nc.scalar.activation(
+            shares[:, PAD:], neg_score[:], ACT.Exp, bias=neg_max[:], scale=-1.0, accum_out=row_sum[:]
+        )
+        lay(0, 0, picked10, 5)
+        inv_sum = sbuf("inv_sum", [P, 1], F32)
         nc.vector.reciprocal(inv_sum[:], row_sum[:])
+        neg_step = work("neg_step")
+        nc.vector.scalar_tensor_tensor(
+            neg_step[:], shares[:, PAD - 1 : PAD - 1 + I], pull_col[:], shares[:, PAD:], ALU.mult, ALU.subtract
+        )
+        picked12 = pick(0, 2, "neg_score")
+        os_bank = bank(3, "os_bank", [P, PACK, P])
+        for t in range(PACK):
+            nc.tensor.transpose(os_bank[:, t, :], os_rows[:, t : t + 1].to_broadcast([P, P]), ident[:])
         factor = work("factor")
         nc.scalar.activation(
             factor[:].rearrange("p (s t) -> p s t", t=PACK),
@@ -180,34 +211,43 @@ def tile_attend_planecos_stepwise_bysign_kernel(
             ACT.Copy,
             scale=inv_sum[:],
         )
-        neg_step = after_gather(1, 2048, "neg_step", [P, I], F32)
-        nc.vector.scalar_tensor_tensor(
-            neg_step[:], shares[:, PAD - 1 : PAD - 1 + I], pull_col[:], shares[:, PAD:], ALU.mult, ALU.subtract
-        )
+        lay(0, 1, picked11, 3)
+        lay(0, 2, picked12, 4)
         w_grouped = sbuf("w_grouped", [P, 2 * Q * PACK], BF16)
         for n, op in enumerate((ALU.min, ALU.max)):
             weights = sbuf("weights%d" % n, [P, I], BF16)
             nc.vector.scalar_tensor_tensor(weights[:], neg_step[:], 0.0, factor[:], op, ALU.mult)
-            w_bank = banks.tile([P, 2, P], F32, name="acc")
-            turn(w_grouped[:, n * Q * PACK : (n + 1) * Q * PACK], weights[:], w_bank[:])
-        values(0, 2)
-        values(0, 3)
-        w_codes = after_gather(3, 0, "w_codes", [P, 2 * Q], U32)
-        w_scales = after_gather(3, 2048, "w_scales", [P, 2 * Q], U8)
-        nc.vector.quantize_mx(out=w_codes[:].bitcast(FP8X4), scales=w_scales[:], in_=w_grouped[:])
+            turn(w_grouped[:, n * Q * PACK : (n + 1) * Q * PACK], weights[:], bank(1 + n, "w_bank%d" % n, [P, 2, P])[:])
+        lay(0, 3, pick(0, 3, "inv_sum"), 0)
 
+        late_codes = sbuf("late_codes", [P, E + 2 * Q], U32, "pool1_3")
+        v2_codes = late_codes[:, :E]
+        v2_scales = sbuf("v2_scales", [P, E], U8)
+        nc.vector.quantize_mx(out=v2_codes.bitcast(FP8X4), scales=v2_scales[:], in_=v_grouped[1][:])
         width = E // 2
-        for part in range(2):
-            cols = slice(part * width, (part + 1) * width)
-            v1_codes = after_gather(3, 4096 + 2048 * part, "v1_codes%d" % part, [P, width], U32)
-            v1_scales = after_gather(3, 5120 + 2048 * part, "v1_scales%d" % part, [P, width], U8)
+        v1_codes = [sbuf("v1_codes%d" % part, [P, width], U32) for part in range(2)]
+        v1_scales = [sbuf("v1_scales%d" % part, [P, width], U8) for part in range(2)]
+
+        def quantize_v1(part):
             nc.vector.quantize_mx(
-                out=v1_codes[:].bitcast(FP8X4),
-                scales=v1_scales[:],
+                out=v1_codes[part][:].bitcast(FP8X4),
+                scales=v1_scales[part][:],
                 in_=v_grouped[0][:, part * width * PACK : (part + 1) * width * PACK],
             )
-            acc = single.tile([P, width], F32, name="result_bank%d" % part)
-            for n, codes, scales in ((1, v2_codes[:, cols], v2_scales[:, cols]), (0, v1_codes[:], v1_scales[:])):
+
+        quantize_v1(0)
+        w_codes = late_codes[:, E:]
+        w_scales = sbuf("w_scales", [P, 2 * Q], U8)
+        nc.vector.quantize_mx(out=w_codes.bitcast(FP8X4), scales=w_scales[:], in_=w_grouped[:])
+        quantize_v1(1)
+
+        for part in range(2):
+            cols = slice(part * width, (part + 1) * width)
+            acc = bank(6 + part, "result_bank%d" % part, [P, width])
+            for n, codes, scales in (
+                (1, v2_codes[:, cols], v2_scales[:, cols]),
+                (0, v1_codes[part][:], v1_scales[part][:]),
+            ):
                 nc.tensor.matmul_mx(
                     out=acc[:],
                     lhsT=w_codes[:, n * Q : (n + 1) * Q].bitcast(FP8X4),

@@ -19,7 +19,7 @@ ACT = mybir.ActivationFunctionType
 P = 128
 PACK = 4
 BANK = 512
-PAD = 8
+CHUNKS = T // BANK
 
 
 def tile_attend_planecos_stepwise_bysign_kernel(
@@ -28,10 +28,14 @@ def tile_attend_planecos_stepwise_bysign_kernel(
     nc = tc.nc
     with ExitStack() as ctx:
         keep = ctx.enter_context(tc.tile_pool(name="keep", bufs=1))
+        reused = ctx.enter_context(tc.tile_pool(name="reused", bufs=1))
         psum = ctx.enter_context(tc.psum_pool(name="psum", bufs=1))
 
         def sbuf(name, shape, dtype, tag=None):
             return keep.tile(shape, dtype, name=name, tag=tag or name, align_bytes=64)
+
+        def over_last_window(name, shape, dtype, at):
+            return reused.tile(shape, dtype, name=name, align_bytes=64, offset=at)
 
         def bank(number, name, shape):
             return psum.tile(shape, F32, name=name, tag="bank%d" % number)
@@ -41,48 +45,54 @@ def tile_attend_planecos_stepwise_bysign_kernel(
 
         key_scales = sbuf("key_scales", [P, BANK], U8)
         nc.gpsimd.memset(key_scales[:].bitcast(I32), 0)
-        warm = sbuf("warm", [P, 1], F32)
-        nc.gpsimd.memset(warm[:], 1.0)
+        four = sbuf("four", [P, 1], F32)
+        nc.gpsimd.memset(four[:], 4.0)
 
-        half = T // 2
-        key_bytes = keys_words[0].rearrange("p n t -> p (n t)")
-        key_words = [sbuf("key_words%d" % n, [P, half], U32) for n in range(2)]
         q_raw = [sbuf("q_raw%d" % n, [P, PACK, Q], F32) for n in range(2)]
+        key_bytes = keys_words[0].rearrange("p n t -> p (n t)")
+        key_front = sbuf("key_front", [P, 2 * BANK], U32)
+        key_back = [sbuf("key_back%d" % n, [P, BANK], U32) for n in range(2)]
+        key_words = [key_front[:, :BANK], key_front[:, BANK:], key_back[0][:], key_back[1][:]]
+
+        def load_keys(tile, first, count):
+            nc.sync.dma_start(
+                out=tile[:].bitcast(I32),
+                in_=key_bytes[:, first * BANK * PACK : (first + count) * BANK * PACK].bitcast(I32),
+            )
+
         nc.sync.dma_start(out=q_raw[0][:], in_=query.rearrange("(p j) w -> p j w", j=PACK))
         for quad in range(4):
             (nc.sync, nc.scalar)[quad % 2].dma_start(
                 out=key_scales[32 * quad : 32 * quad + 16, :].bitcast(I32),
-                in_=keys_scales[0, 4 * quad : 4 * quad + 4, :].rearrange("j (c n) -> c j n", c=4).bitcast(I32),
+                in_=keys_scales[0, 4 * quad : 4 * quad + 4, :].rearrange("j (c n) -> c j n", c=CHUNKS).bitcast(I32),
             )
-        warm_out = sbuf("warm_out", [P, 1], F32)
-        nc.scalar.activation(warm_out[:], warm[:], ACT.Abs_reciprocal_sqrt)
-        for n in range(2):
-            nc.sync.dma_start(
-                out=key_words[n][:].bitcast(I32),
-                in_=key_bytes[:, n * half * PACK : (n + 1) * half * PACK].bitcast(I32),
-            )
+        half = sbuf("half", [P, 1], F32)
+        nc.scalar.activation(half[:], four[:], ACT.Abs_reciprocal_sqrt)
+        load_keys(key_front, 0, 2)
+        load_keys(key_back[0], 2, 1)
         nc.sync.dma_start(out=q_raw[1][:], in_=query2.rearrange("(p j) w -> p j w", j=PACK))
+        load_keys(key_back[1], 3, 1)
 
         lam_col = sbuf("lam_col", [P, 1], F32)
         pull_col = sbuf("pull_col", [P, 1], F32)
-        os_rows = sbuf("os_rows", [P, PACK], F32)
+        factor_rows = sbuf("factor_rows", [P, PACK], F32)
         ident = sbuf("ident", [P, P], F32)
         make_identity(nc, ident[:])
-        nc.gpsimd.dma_start(out=os_rows[:], in_=slot_factor.rearrange("o (p t) -> (o p) t", t=PACK))
+        nc.gpsimd.dma_start(out=factor_rows[:], in_=slot_factor.rearrange("o (p t) -> (o p) t", t=PACK))
         nc.gpsimd.dma_start(out=lam_col[:], in_=lam)
         nc.gpsimd.dma_start(out=pull_col[:], in_=pull)
 
-        lists = [sbuf("list%d" % n, [P, I // 16], U16) for n in range(3)]
-        pool1 = [sbuf("pool1_%d" % n, [P, T], F32) for n in range(4)]
-        pool2 = [sbuf("pool2_%d" % n, [P, X], F32) for n in range(4)]
-        nc.sync.dma_start(out=pool2[0][:], in_=vals2[0:P, :])
-        nc.sync.dma_start(lists[2][:], offs3)
-        nc.sync.dma_start(lists[0][:], offs)
-        nc.sync.dma_start(lists[1][:], offs2)
-        for n in range(1, 4):
-            nc.sync.dma_start(out=pool2[n][:], in_=vals2[n * P : (n + 1) * P, :])
-        for n in range(4):
-            nc.sync.dma_start(out=pool1[n][:], in_=vals[n * P : (n + 1) * P, :])
+        list1, list2, list3 = [sbuf("list%d" % n, [P, I // 16], U16) for n in (1, 2, 3)]
+        pool = [sbuf("pool%d" % n, [P, T], F32) for n in range(3)] + [over_last_window("pool3", [P, T], F32, 0)]
+        store = [sbuf("store%d" % n, [P, X], F32) for n in range(4)]
+        nc.sync.dma_start(list3[:], offs3)
+        nc.sync.dma_start(out=store[0][:], in_=vals2[0:P, :])
+        nc.sync.dma_start(list1[:], offs)
+        nc.sync.dma_start(list2[:], offs2)
+        for n in range(3):
+            nc.sync.dma_start(out=store[n + 1][:], in_=vals2[(n + 1) * P : (n + 2) * P, :])
+            nc.sync.dma_start(out=pool[n][:], in_=vals[n * P : (n + 1) * P, :])
+        nc.sync.dma_start(out=pool[3][:], in_=vals[3 * P :, :])
 
         q_codes, q_scales = [], []
         for n in range(2):
@@ -98,39 +108,42 @@ def tile_attend_planecos_stepwise_bysign_kernel(
 
         planes = [sbuf("plane%d" % n, [P, T], F32) for n in range(2)]
         for n in range(2):
-            for c in range(T // BANK):
-                acc = bank(4 * n + c, "plane_bank%d_%d" % (n, c), [P, BANK])
-                within = (c % 2) * BANK
+            for c in range(CHUNKS):
+                acc = bank(CHUNKS * n + c, "plane_bank%d_%d" % (n, c), [P, BANK])
                 nc.tensor.matmul_mx(
                     out=acc[:],
                     lhsT=q_codes[n][:].bitcast(FP8X4),
                     lhsT_scale=q_scales[n][:],
-                    rhs=key_words[c // 2][:, within : within + BANK].bitcast(FP8X4),
+                    rhs=key_words[c].bitcast(FP8X4),
                     rhs_scale=key_scales[4 * c :, :],
                     start=True,
                     stop=True,
                 )
                 nc.scalar.copy(out=planes[n][:, c * BANK : (c + 1) * BANK], in_=acc[:])
 
-        v_grouped = [sbuf("v_grouped%d" % n, [P, E * PACK], BF16) for n in range(2)]
+        v_codes = over_last_window("v_codes", [P, 2 * E], U32, 4096)
+        v_scales = sbuf("v_scales", [P, 2 * E], U8)
 
-        def turn(dst_bf16, src_bf16, turned):
-            words = src_bf16.bitcast(F32)
+        def pick(picked, window, offsets):
+            nc.vector.tensor_copy(out=picked, in_=window[:].indirect(offsets[:]))
+
+        def pick_on_scalar(picked, window, offsets):
+            nc.scalar.activation(picked, window[:].indirect(offsets[:]), ACT.Copy)
+
+        def turn(turned, picked):
+            words = picked.bitcast(F32)
             for u in range(2):
                 nc.tensor.transpose(turned[:, u, :], words[:, u : I // 2 : 2], ident[:])
+
+        def lay(grouped, turned):
             nc.scalar.copy(
-                out=dst_bf16.bitcast(F32).rearrange("p (r u) -> p r u", u=2), in_=turned.rearrange("p u r -> p r u")
+                out=grouped.bitcast(F32).rearrange("p (b r u) -> p b r u", r=P, u=2),
+                in_=turned.rearrange("p b u r -> p b r u"),
             )
 
-        def pick(n, block, tag=None, into=None):
-            window = (pool1, pool2)[n][block]
-            picked = sbuf("picked%d_%d" % (n, block), [P, I], BF16, tag)[:] if into is None else into
-            nc.vector.tensor_copy(out=picked, in_=window[:].indirect(lists[2 * n][:]))
-            return picked
-
-        def lay(n, block, picked, number):
-            turned = bank(number, "turned%d_%d" % (n, block), [P, 2, P])
-            turn(v_grouped[n][:, block * P * PACK : (block + 1) * P * PACK], picked, turned[:])
+        def quantize_values(place, count, grouped):
+            cols = slice(place * P, (place + count) * P)
+            nc.vector.quantize_mx(out=v_codes[:, cols].bitcast(FP8X4), scales=v_scales[:, cols], in_=grouped)
 
         def add_turned(total, part, first, last):
             for j in range(I // P):
@@ -143,120 +156,143 @@ def tile_attend_planecos_stepwise_bysign_kernel(
                     stop=(last and j == I // P - 1),
                 )
 
-        lay(1, 0, pick(1, 0), 4)
+        first_picked = sbuf("first_picked", [P, I], BF16)
+        pick(first_picked[:], store[0], list3)
+        first_turned = bank(4, "first_turned", [P, 1, 2, P])
+        turn(first_turned[:, 0], first_picked[:])
+        first_grouped = sbuf("first_grouped", [P, I], BF16)
+        lay(first_grouped[:], first_turned[:])
+        narrow2 = sbuf("narrow2", [P, X], BF16)
+        nc.gpsimd.tensor_copy(out=narrow2[:], in_=store[2][:])
 
         la_bank, lb_bank, dot_bank = bank(0, "la_bank", [P, I]), bank(1, "lb_bank", [P, I]), bank(2, "dot_bank", [P, I])
         points = {}
-        for plane, lst in ((0, 0), (0, 1), (1, 0), (1, 1)):
-            point = work("point%d_%d" % (plane, lst))
-            nc.vector.tensor_copy(out=point[:], in_=planes[plane][:].indirect(lists[lst][:]))
-            square = work("square%d_%d" % (plane, lst))
+        for plane, side in ((0, 0), (0, 1), (1, 0), (1, 1)):
+            point = work("point%d_%d" % (plane, side))
+            pick(point[:], planes[plane], (list1, list2)[side])
+            square = work("square%d_%d" % (plane, side))
             nc.scalar.activation(square[:], point[:], ACT.Square)
-            add_turned((la_bank, lb_bank)[lst], square, plane == 0, plane == 1)
-            points[plane, lst] = point
-            if lst == 1:
-                product = work("product%d" % plane)
+            add_turned((la_bank, lb_bank)[side], square, plane == 0, plane == 1)
+            points[plane, side] = point
+            if side == 1:
+                product = work("product%d" % plane, (None, "store2")[plane])
                 nc.gpsimd.tensor_tensor(product[:], points[plane, 0][:], point[:], ALU.mult)
                 add_turned(dot_bank, product, plane == 0, plane == 1)
         la = work("la")
         nc.scalar.copy(out=la[:], in_=la_bank[:])
 
-        pair = sbuf("pair", [P, 2 * I], BF16, "plane1")
-        picked21 = pick(1, 1, into=pair[:, :I])
-        picked22 = pick(1, 2, into=pair[:, I:])
+        narrow3 = sbuf("narrow3", [P, X], BF16, "point1_0")
+        nc.gpsimd.tensor_copy(out=narrow3[:], in_=store[3][:])
+        picked_store2 = sbuf("picked_store2", [P, I], BF16, "square1_0")
+        pick_on_scalar(picked_store2[:], narrow2, list3)
+        pair_a = sbuf("pair_a", [P, 2 * I], BF16, "plane1")
+        pick(pair_a[:, :I], store[1], list3)
+        pick(pair_a[:, I:], pool[0], list1)
         prod = work("prod")
         nc.vector.tensor_tensor(prod[:], lb_bank[:], la[:], ALU.mult)
-        picked23 = pick(1, 3, "square1_1")
-        inv_len = work("inv_len")
-        nc.scalar.activation(inv_len[:], prod[:], ACT.Abs_reciprocal_sqrt, bias=0.5)
-        warm_exp = sbuf("warm_exp", [P, 1], F32)
-        nc.scalar.activation(warm_exp[:], inv_len[:, 0:1], ACT.Exp)
-        lay(1, 1, picked21, 0)
-        lay(1, 2, picked22, 1)
+        picked_pool1 = sbuf("picked_pool1", [P, I], BF16, "square1_1")
+        pick(picked_pool1[:], pool[1], list1)
+        inv_len = work("inv_len", "narrow2")
+        nc.scalar.activation(inv_len[:], prod[:], ACT.Abs_reciprocal_sqrt, bias=half[:])
+        shares = sbuf("shares", [P, P + I], F32)
+        nc.scalar.activation(shares[:, 0:1], inv_len[:, 0:1], ACT.Exp, bias=-1e30)
+        turned_a = bank(0, "turned_a", [P, 2, 2, P])
+        turn(turned_a[:, 0], pair_a[:, :I])
+        turn(turned_a[:, 1], pair_a[:, I:])
+        turned_b = bank(1, "turned_b", [P, 2, 2, P])
+        turn(turned_b[:, 1], picked_store2[:])
+        turn(turned_b[:, 0], picked_pool1[:])
 
-        cosine = work("cosine")
+        cosine = work("cosine", "pool1")
         nc.vector.tensor_tensor(cosine[:], dot_bank[:], inv_len[:], ALU.mult)
-        picked10 = pick(0, 0, "prod")
+        picked_pool2 = sbuf("picked_pool2", [P, I], BF16, "prod")
+        pick(picked_pool2[:], pool[2], list1)
         cos_bank = bank(5, "cos_bank", [P, I])
         add_turned(cos_bank, cosine, True, True)
-        lay(1, 3, picked23, 2)
+        turned_c = bank(2, "turned_c", [P, 2, 2, P])
+        turn(turned_c[:, 0], picked_pool2[:])
+        early_grouped = sbuf("early_grouped", [P, 4 * I], BF16, "narrow2")
+        for pair, turned in enumerate((turned_a, turned_b)):
+            lay(early_grouped[:, 2 * pair * I : 2 * (pair + 1) * I], turned[:])
         neg_lam = sbuf("neg_lam", [P, 1], F32)
         nc.gpsimd.tensor_scalar(neg_lam[:], lam_col[:], -1.0, 0.0, ALU.mult, ALU.add)
-        neg_score = work("neg_score")
+        neg_score = work("neg_score", "pool2")
         neg_max = sbuf("neg_max", [P, 1], F32)
-        nc.vector.tensor_scalar(neg_score[:], cos_bank[:], neg_lam[:], None, ALU.mult, ALU.min, accum_out=neg_max[:])
-        picked11 = pick(0, 1, "cosine")
+        nc.vector.tensor_scalar(
+            neg_score[:].rearrange("p (t s) -> p t s", t=PACK),
+            cos_bank[:].rearrange("p (s t) -> p t s", t=PACK),
+            neg_lam[:],
+            None,
+            ALU.mult,
+            ALU.min,
+            accum_out=neg_max[:],
+        )
+        picked_pool3 = sbuf("picked_pool3", [P, I], BF16, "pool1")
+        pick(picked_pool3[:], pool[3], list1)
+        turn(turned_c[:, 1], picked_pool3[:])
 
-        shares = sbuf("shares", [P, PAD + I], F32)
-        nc.gpsimd.memset(shares[:, PAD - 1 : PAD], 0.0)
         row_sum = sbuf("row_sum", [P, 1], F32)
-        nc.scalar.activation(
-            shares[:, PAD:], neg_score[:], ACT.Exp, bias=neg_max[:], scale=-1.0, accum_out=row_sum[:]
-        )
-        lay(0, 0, picked10, 5)
-        inv_sum = sbuf("inv_sum", [P, 1], F32)
+        nc.scalar.activation(shares[:, P:], neg_score[:], ACT.Exp, bias=neg_max[:], scale=-1.0, accum_out=row_sum[:])
+        nc.scalar.activation(shares[:, 1:P], neg_score[:, I - P : I - 1], ACT.Exp, bias=neg_max[:], scale=-1.0)
+        picked_store3 = sbuf("picked_store3", [P, I], BF16, "neg_lam")
+        pick_on_scalar(picked_store3[:], narrow3, list3)
+        inv_sum = over_last_window("inv_sum", [P, 1], F32, 2048)
         nc.vector.reciprocal(inv_sum[:], row_sum[:])
-        neg_step = work("neg_step")
-        nc.vector.scalar_tensor_tensor(
-            neg_step[:], shares[:, PAD - 1 : PAD - 1 + I], pull_col[:], shares[:, PAD:], ALU.mult, ALU.subtract
-        )
-        picked12 = pick(0, 2, "neg_score")
-        os_bank = bank(3, "os_bank", [P, PACK, P])
-        for t in range(PACK):
-            nc.tensor.transpose(os_bank[:, t, :], os_rows[:, t : t + 1].to_broadcast([P, P]), ident[:])
+        neg_step = over_last_window("neg_step", [P, I], F32, 0)
+        nc.vector.scalar_tensor_tensor(neg_step[:], shares[:, :I], pull_col[:], shares[:, P:], ALU.mult, ALU.subtract)
+        inv_bank = bank(7, "inv_bank", [P, Q])
+        nc.tensor.transpose(inv_bank[:], inv_sum[:].to_broadcast([P, P]), ident[:])
+        step_bank = bank(5, "step_bank", [P, I])
+        add_turned(step_bank, neg_step, True, True)
         factor = work("factor")
-        nc.scalar.activation(
-            factor[:].rearrange("p (s t) -> p s t", t=PACK),
-            os_bank[:].rearrange("p t s -> p s t"),
-            ACT.Copy,
-            scale=inv_sum[:],
+        nc.vector.tensor_tensor(
+            factor[:].rearrange("p (q t) -> p q t", t=PACK),
+            inv_bank[:].unsqueeze(2).broadcast_to([P, Q, PACK]),
+            factor_rows[:].unsqueeze(1).broadcast_to([P, Q, PACK]),
+            ALU.mult,
         )
-        lay(0, 1, picked11, 3)
-        lay(0, 2, picked12, 4)
-        w_grouped = sbuf("w_grouped", [P, 2 * Q * PACK], BF16)
+        w_grouped = [sbuf("w_grouped%d" % n, [P, Q * PACK], BF16) for n in range(2)]
         for n, op in enumerate((ALU.min, ALU.max)):
-            weights = sbuf("weights%d" % n, [P, I], BF16)
-            nc.vector.scalar_tensor_tensor(weights[:], neg_step[:], 0.0, factor[:], op, ALU.mult)
-            turn(w_grouped[:, n * Q * PACK : (n + 1) * Q * PACK], weights[:], bank(1 + n, "w_bank%d" % n, [P, 2, P])[:])
-        lay(0, 3, pick(0, 3, "inv_sum"), 0)
-
-        late_codes = sbuf("late_codes", [P, E + 2 * Q], U32, "pool1_3")
-        v2_codes = late_codes[:, :E]
-        v2_scales = sbuf("v2_scales", [P, E], U8)
-        nc.vector.quantize_mx(out=v2_codes.bitcast(FP8X4), scales=v2_scales[:], in_=v_grouped[1][:])
-        width = E // 2
-        v1_codes = [sbuf("v1_codes%d" % part, [P, width], U32) for part in range(2)]
-        v1_scales = [sbuf("v1_scales%d" % part, [P, width], U8) for part in range(2)]
-
-        def quantize_v1(part):
-            nc.vector.quantize_mx(
-                out=v1_codes[part][:].bitcast(FP8X4),
-                scales=v1_scales[part][:],
-                in_=v_grouped[0][:, part * width * PACK : (part + 1) * width * PACK],
+            nc.vector.scalar_tensor_tensor(
+                w_grouped[n][:].rearrange("p (q t) -> p q t", t=PACK),
+                step_bank[:].rearrange("p (t q) -> p q t", t=PACK),
+                0.0,
+                factor[:].rearrange("p (q t) -> p q t", t=PACK),
+                op,
+                ALU.mult,
             )
+        w_codes = [sbuf("w_codes%d" % n, [P, Q], U32) for n in range(2)]
+        w_scales = [sbuf("w_scales%d" % n, [P, Q], U8) for n in range(2)]
+        for n in range(2):
+            nc.vector.quantize_mx(out=w_codes[n][:].bitcast(FP8X4), scales=w_scales[n][:], in_=w_grouped[n][:])
 
-        quantize_v1(0)
-        w_codes = late_codes[:, E:]
-        w_scales = sbuf("w_scales", [P, 2 * Q], U8)
-        nc.vector.quantize_mx(out=w_codes.bitcast(FP8X4), scales=w_scales[:], in_=w_grouped[:])
-        quantize_v1(1)
+        late_grouped = sbuf("late_grouped", [P, 3 * I], BF16)
+        lay(late_grouped[:, I:], turned_c[:])
+        last_turned = bank(7, "last_turned", [P, 1, 2, P])
+        turn(last_turned[:, 0], picked_store3[:])
+        lay(late_grouped[:, :I], last_turned[:])
 
-        for part in range(2):
-            cols = slice(part * width, (part + 1) * width)
-            acc = bank(6 + part, "result_bank%d" % part, [P, width])
-            for n, codes, scales in (
-                (1, v2_codes[:, cols], v2_scales[:, cols]),
-                (0, v1_codes[part][:], v1_scales[part][:]),
-            ):
+        quantize_values(0, 1, first_grouped[:])
+        for pair in range(2):
+            quantize_values(1 + 2 * pair, 2, early_grouped[:, 2 * pair * I : 2 * (pair + 1) * I])
+        quantize_values(6, 2, late_grouped[:, I:])
+        quantize_values(5, 1, late_grouped[:, :I])
+
+        width = E // 2
+        sums = [bank(number, "sum_bank%d" % number, [P, width]) for number in (3, 6)]
+        for n in range(2):
+            for part in range(2):
+                cols = slice((2 * part + 1 - n) * width, (2 * part + 2 - n) * width)
                 nc.tensor.matmul_mx(
-                    out=acc[:],
-                    lhsT=w_codes[:, n * Q : (n + 1) * Q].bitcast(FP8X4),
-                    lhsT_scale=w_scales[:, n * Q : (n + 1) * Q],
-                    rhs=codes.bitcast(FP8X4),
-                    rhs_scale=scales,
-                    start=(n == 1),
-                    stop=(n == 0),
+                    out=sums[part][:],
+                    lhsT=w_codes[n][:].bitcast(FP8X4),
+                    lhsT_scale=w_scales[n][:],
+                    rhs=v_codes[:, cols].bitcast(FP8X4),
+                    rhs_scale=v_scales[:, cols],
+                    start=(n == 0),
+                    stop=(n == 1),
                 )
+        for part in range(2):
             result = sbuf("result%d" % part, [P, width], F32)
-            nc.scalar.activation(result[:], acc[:], ACT.Copy, scale=-1.0)
-            nc.sync.dma_start(out=out[:, cols], in_=result[:])
+            nc.scalar.activation(result[:], sums[part][:], ACT.Copy, scale=-1.0)
+            nc.sync.dma_start(out=out[:, part * width : (part + 1) * width], in_=result[:])

from contextlib import ExitStack

import concourse.mybir as mybir
from concourse.masks import make_identity

D, T, I, Q, E, X = 512, 2048, 512, 128, 512, 1024
FLOPS = 2 * (2 * D * Q * T + 2 * I * Q * E)

F32 = mybir.dt.float32
BF16 = mybir.dt.bfloat16
I32 = mybir.dt.int32
U32 = mybir.dt.uint32
U16 = mybir.dt.uint16
U8 = mybir.dt.uint8
FP8X4 = mybir.dt.float8_e4m3fn_x4
ALU = mybir.AluOpType
ACT = mybir.ActivationFunctionType

P = 128
PACK = 4
BANK = 512
CHUNKS = T // BANK


def tile_attend_planecos_stepwise_bysign_kernel(
    tc, query, query2, keys_words, keys_scales, lam, pull, slot_factor, vals, vals2, offs, offs2, offs3, out
):
    nc = tc.nc
    with ExitStack() as ctx:
        keep = ctx.enter_context(tc.tile_pool(name="keep", bufs=1))
        reused = ctx.enter_context(tc.tile_pool(name="reused", bufs=1))
        psum = ctx.enter_context(tc.psum_pool(name="psum", bufs=1))

        def sbuf(name, shape, dtype, tag=None):
            return keep.tile(shape, dtype, name=name, tag=tag or name, align_bytes=64)

        def over_last_window(name, shape, dtype, at):
            return reused.tile(shape, dtype, name=name, align_bytes=64, offset=at)

        def bank(number, name, shape):
            return psum.tile(shape, F32, name=name, tag="bank%d" % number)

        def work(name, tag=None):
            return sbuf(name, [P, I], F32, tag)

        key_scales = sbuf("key_scales", [P, BANK], U8)
        nc.gpsimd.memset(key_scales[:].bitcast(I32), 0)
        four = sbuf("four", [P, 1], F32)
        nc.gpsimd.memset(four[:], 4.0)

        q_raw = [sbuf("q_raw%d" % n, [P, PACK, Q], F32) for n in range(2)]
        key_bytes = keys_words[0].rearrange("p n t -> p (n t)")
        key_front = sbuf("key_front", [P, 2 * BANK], U32)
        key_back = [sbuf("key_back%d" % n, [P, BANK], U32) for n in range(2)]
        key_words = [key_front[:, :BANK], key_front[:, BANK:], key_back[0][:], key_back[1][:]]

        def load_keys(tile, first, count):
            nc.sync.dma_start(
                out=tile[:].bitcast(I32),
                in_=key_bytes[:, first * BANK * PACK : (first + count) * BANK * PACK].bitcast(I32),
            )

        nc.sync.dma_start(out=q_raw[0][:], in_=query.rearrange("(p j) w -> p j w", j=PACK))
        for quad in range(4):
            (nc.sync, nc.scalar)[quad % 2].dma_start(
                out=key_scales[32 * quad : 32 * quad + 16, :].bitcast(I32),
                in_=keys_scales[0, 4 * quad : 4 * quad + 4, :].rearrange("j (c n) -> c j n", c=CHUNKS).bitcast(I32),
            )
        half = sbuf("half", [P, 1], F32)
        nc.scalar.activation(half[:], four[:], ACT.Abs_reciprocal_sqrt)
        load_keys(key_front, 0, 2)
        load_keys(key_back[0], 2, 1)
        nc.sync.dma_start(out=q_raw[1][:], in_=query2.rearrange("(p j) w -> p j w", j=PACK))
        load_keys(key_back[1], 3, 1)

        lam_col = sbuf("lam_col", [P, 1], F32)
        pull_col = sbuf("pull_col", [P, 1], F32)
        factor_rows = sbuf("factor_rows", [P, PACK], F32)
        ident = sbuf("ident", [P, P], F32)
        make_identity(nc, ident[:])
        nc.gpsimd.dma_start(out=factor_rows[:], in_=slot_factor.rearrange("o (p t) -> (o p) t", t=PACK))
        nc.gpsimd.dma_start(out=lam_col[:], in_=lam)
        nc.gpsimd.dma_start(out=pull_col[:], in_=pull)

        list1, list2, list3 = [sbuf("list%d" % n, [P, I // 16], U16) for n in (1, 2, 3)]
        pool = [sbuf("pool%d" % n, [P, T], F32) for n in range(3)] + [over_last_window("pool3", [P, T], F32, 0)]
        store = [sbuf("store%d" % n, [P, X], F32) for n in range(4)]
        nc.sync.dma_start(list3[:], offs3)
        nc.sync.dma_start(out=store[0][:], in_=vals2[0:P, :])
        nc.sync.dma_start(list1[:], offs)
        nc.sync.dma_start(list2[:], offs2)
        for n in range(3):
            nc.sync.dma_start(out=store[n + 1][:], in_=vals2[(n + 1) * P : (n + 2) * P, :])
            nc.sync.dma_start(out=pool[n][:], in_=vals[n * P : (n + 1) * P, :])
        nc.sync.dma_start(out=pool[3][:], in_=vals[3 * P :, :])

        q_codes, q_scales = [], []
        for n in range(2):
            grouped = sbuf("q_grouped%d" % n, [P, Q * PACK], BF16)
            nc.vector.tensor_copy(
                out=grouped[:].rearrange("p (w j) -> p w j", j=PACK), in_=q_raw[n][:].rearrange("p j w -> p w j")
            )
            codes = sbuf("q_codes%d" % n, [P, Q], U32)
            scales = sbuf("q_scales%d" % n, [P, Q], U8)
            nc.vector.quantize_mx(out=codes[:].bitcast(FP8X4), scales=scales[:], in_=grouped[:])
            q_codes.append(codes)
            q_scales.append(scales)

        planes = [sbuf("plane%d" % n, [P, T], F32) for n in range(2)]
        for n in range(2):
            for c in range(CHUNKS):
                acc = bank(CHUNKS * n + c, "plane_bank%d_%d" % (n, c), [P, BANK])
                nc.tensor.matmul_mx(
                    out=acc[:],
                    lhsT=q_codes[n][:].bitcast(FP8X4),
                    lhsT_scale=q_scales[n][:],
                    rhs=key_words[c].bitcast(FP8X4),
                    rhs_scale=key_scales[4 * c :, :],
                    start=True,
                    stop=True,
                )
                nc.scalar.copy(out=planes[n][:, c * BANK : (c + 1) * BANK], in_=acc[:])

        v_codes = over_last_window("v_codes", [P, 2 * E], U32, 4096)
        v_scales = sbuf("v_scales", [P, 2 * E], U8)

        def pick(picked, window, offsets):
            nc.vector.tensor_copy(out=picked, in_=window[:].indirect(offsets[:]))

        def pick_on_scalar(picked, window, offsets):
            nc.scalar.activation(picked, window[:].indirect(offsets[:]), ACT.Copy)

        def turn(turned, picked):
            words = picked.bitcast(F32)
            for u in range(2):
                nc.tensor.transpose(turned[:, u, :], words[:, u : I // 2 : 2], ident[:])

        def lay(grouped, turned):
            nc.scalar.copy(
                out=grouped.bitcast(F32).rearrange("p (b r u) -> p b r u", r=P, u=2),
                in_=turned.rearrange("p b u r -> p b r u"),
            )

        def quantize_values(place, count, grouped):
            cols = slice(place * P, (place + count) * P)
            nc.vector.quantize_mx(out=v_codes[:, cols].bitcast(FP8X4), scales=v_scales[:, cols], in_=grouped)

        def add_turned(total, part, first, last):
            for j in range(I // P):
                nc.tensor.matmul(
                    total[:, j * P : (j + 1) * P],
                    lhsT=part[:, j * P : (j + 1) * P],
                    rhs=ident[:],
                    is_transpose=True,
                    start=(first and j == 0),
                    stop=(last and j == I // P - 1),
                )

        first_picked = sbuf("first_picked", [P, I], BF16)
        pick(first_picked[:], store[0], list3)
        first_turned = bank(4, "first_turned", [P, 1, 2, P])
        turn(first_turned[:, 0], first_picked[:])
        first_grouped = sbuf("first_grouped", [P, I], BF16)
        lay(first_grouped[:], first_turned[:])
        narrow2 = sbuf("narrow2", [P, X], BF16)
        nc.gpsimd.tensor_copy(out=narrow2[:], in_=store[2][:])

        la_bank, lb_bank, dot_bank = bank(0, "la_bank", [P, I]), bank(1, "lb_bank", [P, I]), bank(2, "dot_bank", [P, I])
        points = {}
        for plane, side in ((0, 0), (0, 1), (1, 0), (1, 1)):
            point = work("point%d_%d" % (plane, side))
            pick(point[:], planes[plane], (list1, list2)[side])
            square = work("square%d_%d" % (plane, side))
            nc.scalar.activation(square[:], point[:], ACT.Square)
            add_turned((la_bank, lb_bank)[side], square, plane == 0, plane == 1)
            points[plane, side] = point
            if side == 1:
                product = work("product%d" % plane, (None, "store2")[plane])
                nc.gpsimd.tensor_tensor(product[:], points[plane, 0][:], point[:], ALU.mult)
                add_turned(dot_bank, product, plane == 0, plane == 1)
        la = work("la")
        nc.scalar.copy(out=la[:], in_=la_bank[:])

        narrow3 = sbuf("narrow3", [P, X], BF16, "point1_0")
        nc.gpsimd.tensor_copy(out=narrow3[:], in_=store[3][:])
        picked_store2 = sbuf("picked_store2", [P, I], BF16, "square1_0")
        pick_on_scalar(picked_store2[:], narrow2, list3)
        pair_a = sbuf("pair_a", [P, 2 * I], BF16, "plane1")
        pick(pair_a[:, :I], store[1], list3)
        pick(pair_a[:, I:], pool[0], list1)
        prod = work("prod")
        nc.vector.tensor_tensor(prod[:], lb_bank[:], la[:], ALU.mult)
        picked_pool1 = sbuf("picked_pool1", [P, I], BF16, "square1_1")
        pick(picked_pool1[:], pool[1], list1)
        inv_len = work("inv_len", "narrow2")
        nc.scalar.activation(inv_len[:], prod[:], ACT.Abs_reciprocal_sqrt, bias=half[:])
        shares = sbuf("shares", [P, P + I], F32)
        nc.scalar.activation(shares[:, 0:1], inv_len[:, 0:1], ACT.Exp, bias=-1e30)
        turned_a = bank(0, "turned_a", [P, 2, 2, P])
        turn(turned_a[:, 0], pair_a[:, :I])
        turn(turned_a[:, 1], pair_a[:, I:])
        turned_b = bank(1, "turned_b", [P, 2, 2, P])
        turn(turned_b[:, 1], picked_store2[:])
        turn(turned_b[:, 0], picked_pool1[:])

        cosine = work("cosine", "pool1")
        nc.vector.tensor_tensor(cosine[:], dot_bank[:], inv_len[:], ALU.mult)
        picked_pool2 = sbuf("picked_pool2", [P, I], BF16, "prod")
        pick(picked_pool2[:], pool[2], list1)
        cos_bank = bank(5, "cos_bank", [P, I])
        add_turned(cos_bank, cosine, True, True)
        turned_c = bank(2, "turned_c", [P, 2, 2, P])
        turn(turned_c[:, 0], picked_pool2[:])
        early_grouped = sbuf("early_grouped", [P, 4 * I], BF16, "narrow2")
        for pair, turned in enumerate((turned_a, turned_b)):
            lay(early_grouped[:, 2 * pair * I : 2 * (pair + 1) * I], turned[:])
        neg_lam = sbuf("neg_lam", [P, 1], F32)
        nc.gpsimd.tensor_scalar(neg_lam[:], lam_col[:], -1.0, 0.0, ALU.mult, ALU.add)
        neg_score = work("neg_score", "pool2")
        neg_max = sbuf("neg_max", [P, 1], F32)
        nc.vector.tensor_scalar(
            neg_score[:].rearrange("p (t s) -> p t s", t=PACK),
            cos_bank[:].rearrange("p (s t) -> p t s", t=PACK),
            neg_lam[:],
            None,
            ALU.mult,
            ALU.min,
            accum_out=neg_max[:],
        )
        picked_pool3 = sbuf("picked_pool3", [P, I], BF16, "pool1")
        pick(picked_pool3[:], pool[3], list1)
        turn(turned_c[:, 1], picked_pool3[:])

        row_sum = sbuf("row_sum", [P, 1], F32)
        nc.scalar.activation(shares[:, P:], neg_score[:], ACT.Exp, bias=neg_max[:], scale=-1.0, accum_out=row_sum[:])
        nc.scalar.activation(shares[:, 1:P], neg_score[:, I - P : I - 1], ACT.Exp, bias=neg_max[:], scale=-1.0)
        picked_store3 = sbuf("picked_store3", [P, I], BF16, "neg_lam")
        pick_on_scalar(picked_store3[:], narrow3, list3)
        inv_sum = over_last_window("inv_sum", [P, 1], F32, 2048)
        nc.vector.reciprocal(inv_sum[:], row_sum[:])
        neg_step = over_last_window("neg_step", [P, I], F32, 0)
        nc.vector.scalar_tensor_tensor(neg_step[:], shares[:, :I], pull_col[:], shares[:, P:], ALU.mult, ALU.subtract)
        inv_bank = bank(7, "inv_bank", [P, Q])
        nc.tensor.transpose(inv_bank[:], inv_sum[:].to_broadcast([P, P]), ident[:])
        step_bank = bank(5, "step_bank", [P, I])
        add_turned(step_bank, neg_step, True, True)
        factor = work("factor")
        nc.vector.tensor_tensor(
            factor[:].rearrange("p (q t) -> p q t", t=PACK),
            inv_bank[:].unsqueeze(2).broadcast_to([P, Q, PACK]),
            factor_rows[:].unsqueeze(1).broadcast_to([P, Q, PACK]),
            ALU.mult,
        )
        w_grouped = [sbuf("w_grouped%d" % n, [P, Q * PACK], BF16) for n in range(2)]
        for n, op in enumerate((ALU.min, ALU.max)):
            nc.vector.scalar_tensor_tensor(
                w_grouped[n][:].rearrange("p (q t) -> p q t", t=PACK),
                step_bank[:].rearrange("p (t q) -> p q t", t=PACK),
                0.0,
                factor[:].rearrange("p (q t) -> p q t", t=PACK),
                op,
                ALU.mult,
            )
        w_codes = [sbuf("w_codes%d" % n, [P, Q], U32) for n in range(2)]
        w_scales = [sbuf("w_scales%d" % n, [P, Q], U8) for n in range(2)]
        for n in range(2):
            nc.vector.quantize_mx(out=w_codes[n][:].bitcast(FP8X4), scales=w_scales[n][:], in_=w_grouped[n][:])

        late_grouped = sbuf("late_grouped", [P, 3 * I], BF16)
        lay(late_grouped[:, I:], turned_c[:])
        last_turned = bank(7, "last_turned", [P, 1, 2, P])
        turn(last_turned[:, 0], picked_store3[:])
        lay(late_grouped[:, :I], last_turned[:])

        quantize_values(0, 1, first_grouped[:])
        for pair in range(2):
            quantize_values(1 + 2 * pair, 2, early_grouped[:, 2 * pair * I : 2 * (pair + 1) * I])
        quantize_values(6, 2, late_grouped[:, I:])
        quantize_values(5, 1, late_grouped[:, :I])

        width = E // 2
        sums = [bank(number, "sum_bank%d" % number, [P, width]) for number in (3, 6)]
        for n in range(2):
            for part in range(2):
                cols = slice((2 * part + 1 - n) * width, (2 * part + 2 - n) * width)
                nc.tensor.matmul_mx(
                    out=sums[part][:],
                    lhsT=w_codes[n][:].bitcast(FP8X4),
                    lhsT_scale=w_scales[n][:],
                    rhs=v_codes[:, cols].bitcast(FP8X4),
                    rhs_scale=v_scales[:, cols],
                    start=(n == 0),
                    stop=(n == 1),
                )
        for part in range(2):
            result = sbuf("result%d" % part, [P, width], F32)
            nc.scalar.activation(result[:], sums[part][:], ACT.Copy, scale=-1.0)
            nc.sync.dma_start(out=out[:, part * width : (part + 1) * width], in_=result[:])
